import numpy as np
import ml_dtypes


def mxq(x, axis, fmt="e4m3"):
    dtype, down = {"e4m3": (ml_dtypes.float8_e4m3fn, 7), "e5m2": (ml_dtypes.float8_e5m2, 14)}[fmt]
    v = np.moveaxis(np.asarray(x, np.float32).astype(ml_dtypes.bfloat16).astype(np.float64), axis, -1)
    blocks = v.reshape(v.shape[:-1] + (-1, 32))
    amax = np.abs(blocks).max(-1, keepdims=True)
    byte = np.maximum(np.where(amax > 0, np.frexp(amax)[1] - 1 + 127, 0) - down, 1)
    scale = np.exp2(byte - 127.0)
    codes = (blocks / scale).astype(np.float32).astype(dtype).astype(np.float64)
    return np.moveaxis((codes * scale).reshape(v.shape), -1, axis)


WIDE = False


def mx_kscale(k, group=512):
    if not WIDE:
        return np.ones(k)
    levels = np.array([10, -10, 5, -5, 0])
    if group != 512:
        return np.exp2(np.random.permutation(np.resize(levels, k // group))).repeat(group)
    if k % 512:
        return np.exp2(np.random.permutation(np.resize(levels, k // 32))).repeat(32)
    a = np.empty((k // 512, 16))
    for p in range(k // 512):
        a[p, :8] = np.random.permutation(np.resize(levels, 8))
        for g in range(8):
            far = levels[np.abs(levels - a[p, g]) >= 10]
            a[p, g + 8] = far[np.random.randint(len(far))]
    return np.exp2(a.ravel()).repeat(32)


def f64(x):
    return np.asarray(x).astype(np.float64)


G, D, M, O, N = 2, 256, 256, 256, 512


def sgn(shape):
    return np.random.uniform(0.5, 2.0, shape) * np.where(np.random.standard_normal(shape) < 0, -1.0, 1.0)


def setup_inputs():
    n = np.random.standard_normal
    s_d = mx_kscale(D, 0)
    s_m = mx_kscale(M, 0)
    return {
        "x": (n((G, D, N)) * s_d[:, None]).astype(np.float32),
        "w1": (n((G, D, M)) / np.sqrt(D) / s_d[:, None]).astype(np.float32),
        "w2": (n((G, D, M)) / np.sqrt(D) / s_d[:, None]).astype(np.float32),
        "sh": (np.random.uniform(0.1, 0.4, (G, M, 1))).astype(np.float32),
        "d0": (np.random.uniform(2.0, 6.0, (G, M, N))).astype(np.float32),
        "hs": (sgn((G, M, 1)) * s_m[:, None]).astype(np.float32),
        "wo2": (n((G, M, O)) / np.sqrt(M) / s_m[:, None]).astype(np.float32),
        "ob": (0.5 * n((G, O, 1))).astype(np.float32),
        "osc": (np.random.uniform(0.5, 2.0, (G, O, 1))).astype(np.float32),
    }


def reference(x, w1, w2, sh, d0, hs, wo2, ob, osc):
    w1q = mxq(f64(w1), 1, "e4m3")
    xq = mxq(f64(x), 1, "e4m3")
    z1 = w1q.transpose(0, 2, 1) @ xq
    w2q = mxq(f64(w2), 1, "e4m3")
    z2 = w2q.transpose(0, 2, 1) @ xq
    q1 = f64(d0) - z1 * 2.0
    h = np.exp(q1 * f64(sh) * (-1.0)) * z2
    hh = h * f64(hs)
    wo2q = mxq(f64(wo2), 1, "e4m3")
    hhq = mxq(hh, 1, "e4m3")
    y0 = wo2q.transpose(0, 2, 1) @ hhq
    y = np.tanh(y0 + f64(ob)) * f64(osc)
    return y

@@ -1,0 +1,194 @@
+from contextlib import ExitStack
+
+import concourse.mybir as mybir
+
+G, D, M, O, N = 2, 256, 256, 256, 512
+FLOPS = 3 * 2 * G * 256 * 256 * N
+
+F32 = mybir.dt.float32
+BF16 = mybir.dt.bfloat16
+U32 = mybir.dt.uint32
+U8 = mybir.dt.uint8
+FP8X4 = mybir.dt.float8_e4m3fn_x4
+ACT = mybir.ActivationFunctionType
+ALU = mybir.AluOpType
+
+P = 128
+ROWS = 64
+NB = 128
+CHUNKS = N // NB
+X_VECTOR_QUADS = 84
+W1_VECTOR_QUADS = 32
+W2_VECTOR_QUADS = 42
+STORES = [(0, 1), (2,), (3,)]
+
+
+def tile_rows_fkernrbf_kernel(tc, x, w1, w2, sh, d0, hs, wo2, ob, osc, out):
+    nc = tc.nc
+    with ExitStack() as ctx:
+        sb = ctx.enter_context(tc.tile_pool(name="sb", bufs=1))
+        ps = ctx.enter_context(tc.psum_pool(name="ps", bufs=1))
+        ctx.enter_context(tc.manual_schedule())
+
+        def sbuf(name, shape, dtype):
+            return sb.tile(shape, dtype, name=name, align_bytes=64)
+
+        def bank(g, i, name, shape):
+            return ps.tile(shape, F32, name=name, tag="bank_%d_%d" % (g, i))
+
+        def load_rows(name, src):
+            raw = sbuf(name, [P, 4, src.shape[2]], F32)
+            nc.sync.dma_start(out=raw[:], in_=src.rearrange("g (p j) c -> (g p) j c", j=4))
+            return raw
+
+        def load_pairs(name, src, queue):
+            t = sbuf(name, [P, G, 2], F32)
+            queue.dma_start(out=t[:], in_=src.rearrange("g (q b) o -> q g (b o)", b=2))
+            return t
+
+        def copy_on(engine, dst, src):
+            if engine == "vector":
+                nc.vector.tensor_copy(out=dst, in_=src)
+            else:
+                nc.scalar.copy(out=dst, in_=src)
+
+        def interleave(engine, dst, src, lo, hi):
+            copy_on(engine,
+                    dst[:, 4 * lo:4 * hi, :].rearrange("p (c i) j -> p c j i", i=4),
+                    src[:, :, 4 * lo:4 * hi].rearrange("p j (c i) -> p c j i", i=4))
+
+        def interleave_dealt(engine, dst, src, lo, hi):
+            copy_on(engine,
+                    dst[:, :, 2 * lo:2 * hi, :].rearrange("p b (c i) j -> p c j i b", i=2),
+                    src[:, :, 4 * lo:4 * hi].rearrange("p j (c i b) -> p c j i b", i=2, b=2))
+
+        def quantize(codes, scales, grouped, lo, hi):
+            nc.vector.quantize_mx(out=codes[:, lo:hi].bitcast(FP8X4), scales=scales[:, lo:hi],
+                                  in_=grouped[:, 4 * lo:4 * hi])
+
+        def product(dst, g, wq, half, aq, lo):
+            rows = slice(ROWS * g, ROWS * (g + 1))
+            cols = slice(P * half, P * (half + 1))
+            nc.tensor.matmul_mx(out=dst, lhsT=wq[0][rows, cols].bitcast(FP8X4), lhsT_scale=wq[1][rows, cols],
+                                rhs=aq[0][rows, lo:lo + NB].bitcast(FP8X4), rhs_scale=aq[1][rows, lo:lo + NB],
+                                start=True, stop=True)
+
+        def mx_pair(name, width):
+            return (sbuf(name + "_codes", [P, width], U32), sbuf(name + "_scales", [P, width], U8))
+
+        sh_t = load_pairs("sh_t", sh, nc.scalar)
+        hs_t = load_pairs("hs_t", hs, nc.scalar)
+        x_raw = load_rows("x_raw", x)
+        w1_raw = load_rows("w1_raw", w1)
+        w2_raw = load_rows("w2_raw", w2)
+        d0_t = []
+        for b in range(2):
+            t = sbuf("d0_%d" % b, [P, G, N], F32)
+            nc.sync.dma_start(out=t[:], in_=d0.rearrange("g (q b) n -> q g b n", b=2)[:, :, b, :])
+            d0_t.append(t)
+        wo_raw = load_rows("wo_raw", wo2)
+        ob_t = load_pairs("ob_t", ob, nc.sync)
+        osc_t = load_pairs("osc_t", osc, nc.sync)
+
+        warm = sbuf("warm", [P, 1], F32)
+        nc.scalar.activation(out=warm[:], in_=sh_t[:, 0, 0:1], func=ACT.Exp)
+
+        x_bf = sbuf("x_bf", [P, N, 4], BF16)
+        x_flat = x_bf[:].rearrange("p n j -> p (n j)")
+        xq = mx_pair("xq", N)
+        interleave("scalar", x_bf, x_raw, X_VECTOR_QUADS, N // 4)
+        interleave("vector", x_bf, x_raw, 0, 64)
+        interleave("vector", x_bf, x_raw, 64, X_VECTOR_QUADS)
+        quantize(xq[0], xq[1], x_flat, 0, 256)
+        quantize(xq[0], xq[1], x_flat, 256, 512)
+
+        wq = []
+        for name, raw, share in (("w1", w1_raw, W1_VECTOR_QUADS), ("w2", w2_raw, W2_VECTOR_QUADS)):
+            w_bf = sbuf(name + "_bf", [P, 2, P, 4], BF16)
+            q = mx_pair(name + "q", M)
+            interleave_dealt("scalar", w_bf, raw, share, 64)
+            interleave_dealt("vector", w_bf, raw, 0, share)
+            for b in range(2):
+                quantize(q[0], q[1], w_bf[:].rearrange("p b q j -> p (b q j)"), P * b, P * (b + 1))
+            wq.append(q)
+
+        z = {}
+        for w in range(2):
+            for b in range(2):
+                for g in range(G):
+                    z[w, g, b] = bank(g, 2 * w + b, "z_%d_%d_%d" % (w, g, b), [P, N])
+                for s in range(CHUNKS):
+                    for g in range(G):
+                        product(z[w, g, b][:, NB * s:NB * (s + 1)], g, wq[w], b, xq, NB * s)
+
+        e = {}
+        for b in range(2):
+            for g in range(G):
+                t = sbuf("t_%d_%d" % (g, b), [P, N], F32)
+                nc.vector.scalar_tensor_tensor(out=t[:], in0=z[0, g, b][:], scalar=2.0, in1=d0_t[b][:, g, :],
+                                               op0=ALU.mult, op1=ALU.subtract)
+                e[g, b] = sbuf("e_%d_%d" % (g, b), [P, N], F32)
+                nc.scalar.activation(out=e[g, b][:], in_=t[:], func=ACT.Exp, scale=sh_t[:, g, b:b + 1])
+
+        wo_bf = sbuf("wo_bf", [P, 2, P, 4], BF16)
+        woq = mx_pair("woq", O)
+        interleave_dealt("scalar", wo_bf, wo_raw, 0, 64)
+
+        moved = []
+        for s in range(CHUNKS):
+            cols = slice(NB * s, NB * (s + 1))
+            mv = sbuf("moved_%d" % s, [P, 4, NB], BF16)
+            for g in range(G):
+                hh = sbuf("hh_%d_%d" % (s, g), [P, 2, NB], BF16)
+                for b in range(2):
+                    nc.vector.scalar_tensor_tensor(out=hh[:, b, :], in0=z[1, g, b][:, cols],
+                                                   scalar=hs_t[:, g, b:b + 1], in1=e[g, b][:, cols],
+                                                   op0=ALU.mult, op1=ALU.mult)
+                nc.sync.dma_start(out=mv[ROWS * g:ROWS * (g + 1), :, :].rearrange("p (u b) n -> p u (b n)", u=2),
+                                  in_=hh[:].rearrange("q b n -> q (b n)"))
+            moved.append(mv)
+        quantize(woq[0], woq[1], wo_bf[:].rearrange("p b q j -> p (b q j)"), 0, O)
+
+        hh_bf = [sbuf("hh_bf_%d" % s, [P, NB, 4], BF16) for s in range(CHUNKS)]
+        hq = [mx_pair("hq_%d" % s, NB) for s in range(CHUNKS)]
+        th = {}
+        res = {}
+        place = {}
+        for k, group in enumerate(STORES):
+            th[k] = sbuf("th_%d" % k, [P, G, 2, NB * len(group)], F32)
+            res[k] = sbuf("res_%d" % k, [P, G, 2, NB * len(group)], F32)
+            for i, s in enumerate(group):
+                place[s] = (k, i)
+
+        def second_layer(s):
+            quantize(hq[s][0], hq[s][1], hh_bf[s][:].rearrange("p n j -> p (n j)"), 0, NB)
+            y = [bank(g, s, "y_%d_%d" % (g, s), [P, 2, NB]) for g in range(G)]
+            for h in range(2):
+                for g in range(G):
+                    product(y[g][:, h, :], g, woq, h, hq[s], 0)
+            k, i = place[s]
+            for g in range(G):
+                for h in range(2):
+                    nc.scalar.activation(out=th[k][:, g, h, NB * i:NB * (i + 1)], in_=y[g][:, h, :], func=ACT.Tanh,
+                                         bias=ob_t[:, g, h:h + 1])
+
+        def store(k):
+            lo = NB * STORES[k][0]
+            hi = lo + NB * len(STORES[k])
+            for g in range(G):
+                for h in range(2):
+                    nc.vector.tensor_scalar(out=res[k][:, g, h, :], in0=th[k][:, g, h, :],
+                                            scalar1=osc_t[:, g, h:h + 1], scalar2=None, op0=ALU.mult)
+                nc.sync.dma_start(out=out.rearrange("g (q h) n -> q g h n", h=2)[:, g, :, lo:hi],
+                                  in_=res[k][:, g, :, :])
+
+        interleave("scalar", hh_bf[0], moved[0], 0, NB // 4)
+        second_layer(0)
+        interleave("vector", hh_bf[1], moved[1], 0, NB // 4)
+        interleave("vector", hh_bf[2], moved[2], 0, NB // 4)
+        second_layer(1)
+        interleave("vector", hh_bf[3], moved[3], 0, NB // 4)
+        second_layer(2)
+        second_layer(3)
+        for k in range(len(STORES)):
+            store(k)

@@ -17,10 +17,12 @@ P = 128
 ROWS = 64
 NB = 128
 CHUNKS = N // NB
-X_VECTOR_QUADS = 84
-W1_VECTOR_QUADS = 32
-W2_VECTOR_QUADS = 42
+W1_VECTOR_QUADS = 42
 STORES = [(0, 1), (2,), (3,)]
+WARM_EARLY = 20
+WARM_LATE = 24
+WARM_BETWEEN = 50
+HH_VECTOR_QUADS = 20
 
 
 def tile_rows_fkernrbf_kernel(tc, x, w1, w2, sh, d0, hs, wo2, ob, osc, out):
@@ -41,10 +43,6 @@ def tile_rows_fkernrbf_kernel(tc, x, w1, w2, sh, d0, hs, wo2, ob, osc, out):
             nc.sync.dma_start(out=raw[:], in_=src.rearrange("g (p j) c -> (g p) j c", j=4))
             return raw
 
-        def load_pairs(name, src, queue):
-            t = sbuf(name, [P, G, 2], F32)
-            queue.dma_start(out=t[:], in_=src.rearrange("g (q b) o -> q g (b o)", b=2))
-            return t
 
         def copy_on(engine, dst, src):
             if engine == "vector":
@@ -76,78 +74,131 @@ def tile_rows_fkernrbf_kernel(tc, x, w1, w2, sh, d0, hs, wo2, ob, osc, out):
         def mx_pair(name, width):
             return (sbuf(name + "_codes", [P, width], U32), sbuf(name + "_scales", [P, width], U8))
 
-        sh_t = load_pairs("sh_t", sh, nc.scalar)
-        hs_t = load_pairs("hs_t", hs, nc.scalar)
-        x_raw = load_rows("x_raw", x)
+        rows_t = sbuf("rows_t", [P, 64], F32)
+        nc.gpsimd.memset(rows_t[:], 0.0)
         w1_raw = load_rows("w1_raw", w1)
+        for v, vec in enumerate((sh, hs, ob, osc)):
+            nc.sync.dma_start(out=rows_t[v:P:16, :], in_=vec.rearrange("g (i c) o -> i g (c o)", i=4))
+        x_raw = load_rows("x_raw", x)
         w2_raw = load_rows("w2_raw", w2)
-        d0_t = []
-        for b in range(2):
-            t = sbuf("d0_%d" % b, [P, G, N], F32)
-            nc.sync.dma_start(out=t[:], in_=d0.rearrange("g (q b) n -> q g b n", b=2)[:, :, b, :])
-            d0_t.append(t)
-        wo_raw = load_rows("wo_raw", wo2)
-        ob_t = load_pairs("ob_t", ob, nc.sync)
-        osc_t = load_pairs("osc_t", osc, nc.sync)
-
-        warm = sbuf("warm", [P, 1], F32)
-        nc.scalar.activation(out=warm[:], in_=sh_t[:, 0, 0:1], func=ACT.Exp)
-
-        x_bf = sbuf("x_bf", [P, N, 4], BF16)
-        x_flat = x_bf[:].rearrange("p n j -> p (n j)")
-        xq = mx_pair("xq", N)
-        interleave("scalar", x_bf, x_raw, X_VECTOR_QUADS, N // 4)
-        interleave("vector", x_bf, x_raw, 0, 64)
-        interleave("vector", x_bf, x_raw, 64, X_VECTOR_QUADS)
-        quantize(xq[0], xq[1], x_flat, 0, 256)
-        quantize(xq[0], xq[1], x_flat, 256, 512)
-
-        wq = []
-        for name, raw, share in (("w1", w1_raw, W1_VECTOR_QUADS), ("w2", w2_raw, W2_VECTOR_QUADS)):
-            w_bf = sbuf(name + "_bf", [P, 2, P, 4], BF16)
-            q = mx_pair(name + "q", M)
-            interleave_dealt("scalar", w_bf, raw, share, 64)
-            interleave_dealt("vector", w_bf, raw, 0, share)
-            for b in range(2):
-                quantize(q[0], q[1], w_bf[:].rearrange("p b q j -> p (b q j)"), P * b, P * (b + 1))
-            wq.append(q)
-
-        z = {}
-        for w in range(2):
-            for b in range(2):
-                for g in range(G):
-                    z[w, g, b] = bank(g, 2 * w + b, "z_%d_%d_%d" % (w, g, b), [P, N])
-                for s in range(CHUNKS):
-                    for g in range(G):
-                        product(z[w, g, b][:, NB * s:NB * (s + 1)], g, wq[w], b, xq, NB * s)
-
-        e = {}
+        d0_t = {}
         for b in range(2):
             for g in range(G):
+                d0_t[g, b] = sbuf("d0_%d_%d" % (g, b), [P, N], F32)
+                nc.sync.dma_start(out=d0_t[g, b][:], in_=d0.rearrange("g (q b) n -> q g b n", b=2)[:, g, b, :])
+        wo_raw = load_rows("wo_raw", wo2)
+
+        ones = sbuf("ones", [P, 4 * P], BF16)
+        nc.vector.memset(ones[:], 1.0)
+        oq = mx_pair("oq", P)
+        quantize(oq[0], oq[1], ones, 0, P)
+        warm_bank = ps.tile([P, NB], F32, name="warm_bank", tag="warm_bank")
+
+        def warm_up(q, count):
+            for i in range(count):
+                nc.tensor.matmul_mx(out=warm_bank[:], lhsT=q[0][:, 0:P].bitcast(FP8X4), lhsT_scale=q[1][:, 0:P],
+                                    rhs=q[0][:, 0:NB].bitcast(FP8X4), rhs_scale=q[1][:, 0:NB], start=True, stop=True)
+
+        warm_up(oq, WARM_EARLY)
+
+        warm = sbuf("warm", [P, 1], F32)
+        nc.scalar.activation(out=warm[:], in_=ones[:, 0:1], func=ACT.Exp)
+
+        split_t = sbuf("split_t", [P, 2, 32], F32)
+        cols_t = sbuf("cols_t", [P, 2, 32], F32)
+
+        def column(v, g, b):
+            return cols_t[:, b, 16 * g + v:16 * g + v + 1]
+
+        w_bf = [sbuf("w%d_bf" % w, [P, 2, P, 4], BF16) for w in range(2)]
+        w_flat = [t[:].rearrange("p b q j -> p (b q j)") for t in w_bf]
+        wq = [mx_pair("w%dq" % w, M) for w in range(2)]
+        interleave_dealt("scalar", w_bf[0], w1_raw, W1_VECTOR_QUADS, 64)
+        interleave_dealt("vector", w_bf[0], w1_raw, 0, W1_VECTOR_QUADS)
+        nc.vector.tensor_copy(out=split_t[:], in_=rows_t[:].rearrange("p (a b) -> p b a", b=2))
+        quantize(wq[0][0], wq[0][1], w_flat[0], 0, M)
+        for b in range(2):
+            nc.vector.transpose(out=cols_t[:, b, :], in_=split_t[:, b, :])
+        warm_up(wq[0], WARM_LATE)
+
+        x_bf = [sbuf("x_bf_%d" % s, [P, NB, 4], BF16) for s in range(CHUNKS)]
+        xq = [mx_pair("xq_%d" % s, NB) for s in range(CHUNKS)]
+
+        def x_interleave(engine, s):
+            interleave(engine, x_bf[s], x_raw[:, :, NB * s:NB * (s + 1)], 0, NB // 4)
+
+        def x_quantize(s):
+            quantize(xq[s][0], xq[s][1], x_bf[s][:].rearrange("p n j -> p (n j)"), 0, NB)
+
+        x_interleave("scalar", 1)
+        x_interleave("scalar", 3)
+        x_interleave("vector", 0)
+        x_interleave("vector", 2)
+        for s in range(CHUNKS):
+            x_quantize(s)
+        interleave_dealt("scalar", w_bf[1], w2_raw, 0, 64)
+
+        z1 = {}
+        for b in range(2):
+            for g in range(G):
+                z1[g, b] = bank(g, b, "z1_%d_%d" % (g, b), [P, N])
+            for s in range(CHUNKS):
+                for g in range(G):
+                    product(z1[g, b][:, NB * s:NB * (s + 1)], g, wq[0], b, xq[s], 0)
+
+        z2 = {}
+        e = {}
+
+        def second_product(k, i):
+            for g in range(G):
+                z2[g, k] = bank(g, i, "z2_%d_%d" % (g, k), [P, 2, 2, NB])
+            for b in range(2):
+                for u in range(2):
+                    for g in range(G):
+                        product(z2[g, k][:, b, u, :], g, wq[1], b, xq[2 * k + u], 0)
+
+        def kernel_values(b):
+            for g in range(G):
                 t = sbuf("t_%d_%d" % (g, b), [P, N], F32)
-                nc.vector.scalar_tensor_tensor(out=t[:], in0=z[0, g, b][:], scalar=2.0, in1=d0_t[b][:, g, :],
+                nc.vector.scalar_tensor_tensor(out=t[:], in0=z1[g, b][:], scalar=2.0, in1=d0_t[g, b][:],
                                                op0=ALU.mult, op1=ALU.subtract)
                 e[g, b] = sbuf("e_%d_%d" % (g, b), [P, N], F32)
-                nc.scalar.activation(out=e[g, b][:], in_=t[:], func=ACT.Exp, scale=sh_t[:, g, b:b + 1])
+                nc.scalar.activation(out=e[g, b][:], in_=t[:], func=ACT.Exp, scale=column(0, g, b))
+
+        kernel_values(0)
+        quantize(wq[1][0], wq[1][1], w_flat[1], 0, M)
+        second_product(0, 2)
+        second_product(1, 0)
+        warm_up(wq[1], WARM_BETWEEN)
+        kernel_values(1)
 
         wo_bf = sbuf("wo_bf", [P, 2, P, 4], BF16)
         woq = mx_pair("woq", O)
         interleave_dealt("scalar", wo_bf, wo_raw, 0, 64)
 
-        moved = []
+        moved = [sbuf("moved_%d" % s, [P, 4, NB], BF16) for s in range(CHUNKS)]
+        hh = {}
         for s in range(CHUNKS):
-            cols = slice(NB * s, NB * (s + 1))
-            mv = sbuf("moved_%d" % s, [P, 4, NB], BF16)
             for g in range(G):
-                hh = sbuf("hh_%d_%d" % (s, g), [P, 2, NB], BF16)
+                hh[s, g] = sbuf("hh_%d_%d" % (s, g), [P, 2, NB], BF16)
+
+        def hidden(s, g, b):
+            nc.vector.scalar_tensor_tensor(out=hh[s, g][:, b, :], in0=z2[g, s // 2][:, b, s % 2, :],
+                                           scalar=column(1, g, b), in1=e[g, b][:, NB * s:NB * (s + 1)],
+                                           op0=ALU.mult, op1=ALU.mult)
+            if b == 1:
+                nc.sync.dma_start(
+                    out=moved[s][ROWS * g:ROWS * (g + 1), :, :].rearrange("p (u b) n -> p u (b n)", u=2),
+                    in_=hh[s, g][:].rearrange("q b n -> q (b n)"))
+
+        for g in range(G):
+            for s in range(2):
                 for b in range(2):
-                    nc.vector.scalar_tensor_tensor(out=hh[:, b, :], in0=z[1, g, b][:, cols],
-                                                   scalar=hs_t[:, g, b:b + 1], in1=e[g, b][:, cols],
-                                                   op0=ALU.mult, op1=ALU.mult)
-                nc.sync.dma_start(out=mv[ROWS * g:ROWS * (g + 1), :, :].rearrange("p (u b) n -> p u (b n)", u=2),
-                                  in_=hh[:].rearrange("q b n -> q (b n)"))
-            moved.append(mv)
-        quantize(woq[0], woq[1], wo_bf[:].rearrange("p b q j -> p (b q j)"), 0, O)
+                    hidden(s, g, b)
+        for s in range(2, CHUNKS):
+            for g in range(G):
+                for b in range(2):
+                    hidden(s, g, b)
 
         hh_bf = [sbuf("hh_bf_%d" % s, [P, NB, 4], BF16) for s in range(CHUNKS)]
         hq = [mx_pair("hq_%d" % s, NB) for s in range(CHUNKS)]
@@ -162,7 +213,7 @@ def tile_rows_fkernrbf_kernel(tc, x, w1, w2, sh, d0, hs, wo2, ob, osc, out):
 
         def second_layer(s):
             quantize(hq[s][0], hq[s][1], hh_bf[s][:].rearrange("p n j -> p (n j)"), 0, NB)
-            y = [bank(g, s, "y_%d_%d" % (g, s), [P, 2, NB]) for g in range(G)]
+            y = [bank(g, (1, 2, 0, 1)[s], "y_%d_%d" % (g, s), [P, 2, NB]) for g in range(G)]
             for h in range(2):
                 for g in range(G):
                     product(y[g][:, h, :], g, woq, h, hq[s], 0)
@@ -170,7 +221,7 @@ def tile_rows_fkernrbf_kernel(tc, x, w1, w2, sh, d0, hs, wo2, ob, osc, out):
             for g in range(G):
                 for h in range(2):
                     nc.scalar.activation(out=th[k][:, g, h, NB * i:NB * (i + 1)], in_=y[g][:, h, :], func=ACT.Tanh,
-                                         bias=ob_t[:, g, h:h + 1])
+                                         bias=column(2, g, h))
 
         def store(k):
             lo = NB * STORES[k][0]
@@ -178,17 +229,17 @@ def tile_rows_fkernrbf_kernel(tc, x, w1, w2, sh, d0, hs, wo2, ob, osc, out):
             for g in range(G):
                 for h in range(2):
                     nc.vector.tensor_scalar(out=res[k][:, g, h, :], in0=th[k][:, g, h, :],
-                                            scalar1=osc_t[:, g, h:h + 1], scalar2=None, op0=ALU.mult)
+                                            scalar1=column(3, g, h), scalar2=None, op0=ALU.mult)
                 nc.sync.dma_start(out=out.rearrange("g (q h) n -> q g h n", h=2)[:, g, :, lo:hi],
                                   in_=res[k][:, g, :, :])
 
-        interleave("scalar", hh_bf[0], moved[0], 0, NB // 4)
-        second_layer(0)
-        interleave("vector", hh_bf[1], moved[1], 0, NB // 4)
-        interleave("vector", hh_bf[2], moved[2], 0, NB // 4)
-        second_layer(1)
-        interleave("vector", hh_bf[3], moved[3], 0, NB // 4)
-        second_layer(2)
-        second_layer(3)
+        for s in range(2):
+            interleave("scalar", hh_bf[s], moved[s], HH_VECTOR_QUADS, NB // 4)
+        quantize(woq[0], woq[1], wo_bf[:].rearrange("p b q j -> p (b q j)"), 0, O)
+        for pair in ((0, 1), (2, 3)):
+            for s in pair:
+                interleave("vector", hh_bf[s], moved[s], 0, HH_VECTOR_QUADS if s < 2 else NB // 4)
+            for s in pair:
+                second_layer(s)
         for k in range(len(STORES)):
             store(k)

@@ -19,9 +19,6 @@ NB = 128
 CHUNKS = N // NB
 W1_VECTOR_QUADS = 42
 STORES = [(0, 1), (2,), (3,)]
-WARM_EARLY = 20
-WARM_LATE = 24
-WARM_BETWEEN = 50
 HH_VECTOR_QUADS = 20
 
 
@@ -57,8 +54,8 @@ def tile_rows_fkernrbf_kernel(tc, x, w1, w2, sh, d0, hs, wo2, ob, osc, out):
 
         def interleave_dealt(engine, dst, src, lo, hi):
             copy_on(engine,
-                    dst[:, :, 2 * lo:2 * hi, :].rearrange("p b (c i) j -> p c j i b", i=2),
-                    src[:, :, 4 * lo:4 * hi].rearrange("p j (c i b) -> p c j i b", i=2, b=2))
+                    dst[:, :, 2 * lo:2 * hi, :].rearrange("p b (c i) j -> p c b i j", i=2),
+                    src[:, :, 4 * lo:4 * hi].rearrange("p j (c i b) -> p c b i j", i=2, b=2))
 
         def quantize(codes, scales, grouped, lo, hi):
             nc.vector.quantize_mx(out=codes[:, lo:hi].bitcast(FP8X4), scales=scales[:, lo:hi],
@@ -88,22 +85,6 @@ def tile_rows_fkernrbf_kernel(tc, x, w1, w2, sh, d0, hs, wo2, ob, osc, out):
                 nc.sync.dma_start(out=d0_t[g, b][:], in_=d0.rearrange("g (q b) n -> q g b n", b=2)[:, g, b, :])
         wo_raw = load_rows("wo_raw", wo2)
 
-        ones = sbuf("ones", [P, 4 * P], BF16)
-        nc.vector.memset(ones[:], 1.0)
-        oq = mx_pair("oq", P)
-        quantize(oq[0], oq[1], ones, 0, P)
-        warm_bank = ps.tile([P, NB], F32, name="warm_bank", tag="warm_bank")
-
-        def warm_up(q, count):
-            for i in range(count):
-                nc.tensor.matmul_mx(out=warm_bank[:], lhsT=q[0][:, 0:P].bitcast(FP8X4), lhsT_scale=q[1][:, 0:P],
-                                    rhs=q[0][:, 0:NB].bitcast(FP8X4), rhs_scale=q[1][:, 0:NB], start=True, stop=True)
-
-        warm_up(oq, WARM_EARLY)
-
-        warm = sbuf("warm", [P, 1], F32)
-        nc.scalar.activation(out=warm[:], in_=ones[:, 0:1], func=ACT.Exp)
-
         split_t = sbuf("split_t", [P, 2, 32], F32)
         cols_t = sbuf("cols_t", [P, 2, 32], F32)
 
@@ -119,7 +100,6 @@ def tile_rows_fkernrbf_kernel(tc, x, w1, w2, sh, d0, hs, wo2, ob, osc, out):
         quantize(wq[0][0], wq[0][1], w_flat[0], 0, M)
         for b in range(2):
             nc.vector.transpose(out=cols_t[:, b, :], in_=split_t[:, b, :])
-        warm_up(wq[0], WARM_LATE)
 
         x_bf = [sbuf("x_bf_%d" % s, [P, NB, 4], BF16) for s in range(CHUNKS)]
         xq = [mx_pair("xq_%d" % s, NB) for s in range(CHUNKS)]
@@ -168,8 +148,7 @@ def tile_rows_fkernrbf_kernel(tc, x, w1, w2, sh, d0, hs, wo2, ob, osc, out):
         kernel_values(0)
         quantize(wq[1][0], wq[1][1], w_flat[1], 0, M)
         second_product(0, 2)
-        second_product(1, 0)
-        warm_up(wq[1], WARM_BETWEEN)
+        second_product(1, 3)
         kernel_values(1)
 
         wo_bf = sbuf("wo_bf", [P, 2, P, 4], BF16)
@@ -213,7 +192,7 @@ def tile_rows_fkernrbf_kernel(tc, x, w1, w2, sh, d0, hs, wo2, ob, osc, out):
 
         def second_layer(s):
             quantize(hq[s][0], hq[s][1], hh_bf[s][:].rearrange("p n j -> p (n j)"), 0, NB)
-            y = [bank(g, (1, 2, 0, 1)[s], "y_%d_%d" % (g, s), [P, 2, NB]) for g in range(G)]
+            y = [bank(g, s, "y_%d_%d" % (g, s), [P, 2, NB]) for g in range(G)]
             for h in range(2):
                 for g in range(G):
                     product(y[g][:, h, :], g, woq, h, hq[s], 0)

from contextlib import ExitStack

import concourse.mybir as mybir

G, D, M, O, N = 2, 256, 256, 256, 512
FLOPS = 3 * 2 * G * 256 * 256 * N

F32 = mybir.dt.float32
BF16 = mybir.dt.bfloat16
U32 = mybir.dt.uint32
U8 = mybir.dt.uint8
FP8X4 = mybir.dt.float8_e4m3fn_x4
ACT = mybir.ActivationFunctionType
ALU = mybir.AluOpType

P = 128
ROWS = 64
NB = 128
CHUNKS = N // NB
W1_VECTOR_QUADS = 42
STORES = [(0, 1), (2,), (3,)]
HH_VECTOR_QUADS = 20


def tile_rows_fkernrbf_kernel(tc, x, w1, w2, sh, d0, hs, wo2, ob, osc, out):
    nc = tc.nc
    with ExitStack() as ctx:
        sb = ctx.enter_context(tc.tile_pool(name="sb", bufs=1))
        ps = ctx.enter_context(tc.psum_pool(name="ps", bufs=1))
        ctx.enter_context(tc.manual_schedule())

        def sbuf(name, shape, dtype):
            return sb.tile(shape, dtype, name=name, align_bytes=64)

        def bank(g, i, name, shape):
            return ps.tile(shape, F32, name=name, tag="bank_%d_%d" % (g, i))

        def load_rows(name, src):
            raw = sbuf(name, [P, 4, src.shape[2]], F32)
            nc.sync.dma_start(out=raw[:], in_=src.rearrange("g (p j) c -> (g p) j c", j=4))
            return raw


        def copy_on(engine, dst, src):
            if engine == "vector":
                nc.vector.tensor_copy(out=dst, in_=src)
            else:
                nc.scalar.copy(out=dst, in_=src)

        def interleave(engine, dst, src, lo, hi):
            copy_on(engine,
                    dst[:, 4 * lo:4 * hi, :].rearrange("p (c i) j -> p c j i", i=4),
                    src[:, :, 4 * lo:4 * hi].rearrange("p j (c i) -> p c j i", i=4))

        def interleave_dealt(engine, dst, src, lo, hi):
            copy_on(engine,
                    dst[:, :, 2 * lo:2 * hi, :].rearrange("p b (c i) j -> p c b i j", i=2),
                    src[:, :, 4 * lo:4 * hi].rearrange("p j (c i b) -> p c b i j", i=2, b=2))

        def quantize(codes, scales, grouped, lo, hi):
            nc.vector.quantize_mx(out=codes[:, lo:hi].bitcast(FP8X4), scales=scales[:, lo:hi],
                                  in_=grouped[:, 4 * lo:4 * hi])

        def product(dst, g, wq, half, aq, lo):
            rows = slice(ROWS * g, ROWS * (g + 1))
            cols = slice(P * half, P * (half + 1))
            nc.tensor.matmul_mx(out=dst, lhsT=wq[0][rows, cols].bitcast(FP8X4), lhsT_scale=wq[1][rows, cols],
                                rhs=aq[0][rows, lo:lo + NB].bitcast(FP8X4), rhs_scale=aq[1][rows, lo:lo + NB],
                                start=True, stop=True)

        def mx_pair(name, width):
            return (sbuf(name + "_codes", [P, width], U32), sbuf(name + "_scales", [P, width], U8))

        rows_t = sbuf("rows_t", [P, 64], F32)
        nc.gpsimd.memset(rows_t[:], 0.0)
        w1_raw = load_rows("w1_raw", w1)
        for v, vec in enumerate((sh, hs, ob, osc)):
            nc.sync.dma_start(out=rows_t[v:P:16, :], in_=vec.rearrange("g (i c) o -> i g (c o)", i=4))
        x_raw = load_rows("x_raw", x)
        w2_raw = load_rows("w2_raw", w2)
        d0_t = {}
        for b in range(2):
            for g in range(G):
                d0_t[g, b] = sbuf("d0_%d_%d" % (g, b), [P, N], F32)
                nc.sync.dma_start(out=d0_t[g, b][:], in_=d0.rearrange("g (q b) n -> q g b n", b=2)[:, g, b, :])
        wo_raw = load_rows("wo_raw", wo2)

        split_t = sbuf("split_t", [P, 2, 32], F32)
        cols_t = sbuf("cols_t", [P, 2, 32], F32)

        def column(v, g, b):
            return cols_t[:, b, 16 * g + v:16 * g + v + 1]

        w_bf = [sbuf("w%d_bf" % w, [P, 2, P, 4], BF16) for w in range(2)]
        w_flat = [t[:].rearrange("p b q j -> p (b q j)") for t in w_bf]
        wq = [mx_pair("w%dq" % w, M) for w in range(2)]
        interleave_dealt("scalar", w_bf[0], w1_raw, W1_VECTOR_QUADS, 64)
        interleave_dealt("vector", w_bf[0], w1_raw, 0, W1_VECTOR_QUADS)
        nc.vector.tensor_copy(out=split_t[:], in_=rows_t[:].rearrange("p (a b) -> p b a", b=2))
        quantize(wq[0][0], wq[0][1], w_flat[0], 0, M)
        for b in range(2):
            nc.vector.transpose(out=cols_t[:, b, :], in_=split_t[:, b, :])

        x_bf = [sbuf("x_bf_%d" % s, [P, NB, 4], BF16) for s in range(CHUNKS)]
        xq = [mx_pair("xq_%d" % s, NB) for s in range(CHUNKS)]

        def x_interleave(engine, s):
            interleave(engine, x_bf[s], x_raw[:, :, NB * s:NB * (s + 1)], 0, NB // 4)

        def x_quantize(s):
            quantize(xq[s][0], xq[s][1], x_bf[s][:].rearrange("p n j -> p (n j)"), 0, NB)

        x_interleave("scalar", 1)
        x_interleave("scalar", 3)
        x_interleave("vector", 0)
        x_interleave("vector", 2)
        for s in range(CHUNKS):
            x_quantize(s)
        interleave_dealt("scalar", w_bf[1], w2_raw, 0, 64)

        z1 = {}
        for b in range(2):
            for g in range(G):
                z1[g, b] = bank(g, b, "z1_%d_%d" % (g, b), [P, N])
            for s in range(CHUNKS):
                for g in range(G):
                    product(z1[g, b][:, NB * s:NB * (s + 1)], g, wq[0], b, xq[s], 0)

        z2 = {}
        e = {}

        def second_product(k, i):
            for g in range(G):
                z2[g, k] = bank(g, i, "z2_%d_%d" % (g, k), [P, 2, 2, NB])
            for b in range(2):
                for u in range(2):
                    for g in range(G):
                        product(z2[g, k][:, b, u, :], g, wq[1], b, xq[2 * k + u], 0)

        def kernel_values(b):
            for g in range(G):
                t = sbuf("t_%d_%d" % (g, b), [P, N], F32)
                nc.vector.scalar_tensor_tensor(out=t[:], in0=z1[g, b][:], scalar=2.0, in1=d0_t[g, b][:],
                                               op0=ALU.mult, op1=ALU.subtract)
                e[g, b] = sbuf("e_%d_%d" % (g, b), [P, N], F32)
                nc.scalar.activation(out=e[g, b][:], in_=t[:], func=ACT.Exp, scale=column(0, g, b))

        kernel_values(0)
        quantize(wq[1][0], wq[1][1], w_flat[1], 0, M)
        second_product(0, 2)
        second_product(1, 3)
        kernel_values(1)

        wo_bf = sbuf("wo_bf", [P, 2, P, 4], BF16)
        woq = mx_pair("woq", O)
        interleave_dealt("scalar", wo_bf, wo_raw, 0, 64)

        moved = [sbuf("moved_%d" % s, [P, 4, NB], BF16) for s in range(CHUNKS)]
        hh = {}
        for s in range(CHUNKS):
            for g in range(G):
                hh[s, g] = sbuf("hh_%d_%d" % (s, g), [P, 2, NB], BF16)

        def hidden(s, g, b):
            nc.vector.scalar_tensor_tensor(out=hh[s, g][:, b, :], in0=z2[g, s // 2][:, b, s % 2, :],
                                           scalar=column(1, g, b), in1=e[g, b][:, NB * s:NB * (s + 1)],
                                           op0=ALU.mult, op1=ALU.mult)
            if b == 1:
                nc.sync.dma_start(
                    out=moved[s][ROWS * g:ROWS * (g + 1), :, :].rearrange("p (u b) n -> p u (b n)", u=2),
                    in_=hh[s, g][:].rearrange("q b n -> q (b n)"))

        for g in range(G):
            for s in range(2):
                for b in range(2):
                    hidden(s, g, b)
        for s in range(2, CHUNKS):
            for g in range(G):
                for b in range(2):
                    hidden(s, g, b)

        hh_bf = [sbuf("hh_bf_%d" % s, [P, NB, 4], BF16) for s in range(CHUNKS)]
        hq = [mx_pair("hq_%d" % s, NB) for s in range(CHUNKS)]
        th = {}
        res = {}
        place = {}
        for k, group in enumerate(STORES):
            th[k] = sbuf("th_%d" % k, [P, G, 2, NB * len(group)], F32)
            res[k] = sbuf("res_%d" % k, [P, G, 2, NB * len(group)], F32)
            for i, s in enumerate(group):
                place[s] = (k, i)

        def second_layer(s):
            quantize(hq[s][0], hq[s][1], hh_bf[s][:].rearrange("p n j -> p (n j)"), 0, NB)
            y = [bank(g, s, "y_%d_%d" % (g, s), [P, 2, NB]) for g in range(G)]
            for h in range(2):
                for g in range(G):
                    product(y[g][:, h, :], g, woq, h, hq[s], 0)
            k, i = place[s]
            for g in range(G):
                for h in range(2):
                    nc.scalar.activation(out=th[k][:, g, h, NB * i:NB * (i + 1)], in_=y[g][:, h, :], func=ACT.Tanh,
                                         bias=column(2, g, h))

        def store(k):
            lo = NB * STORES[k][0]
            hi = lo + NB * len(STORES[k])
            for g in range(G):
                for h in range(2):
                    nc.vector.tensor_scalar(out=res[k][:, g, h, :], in0=th[k][:, g, h, :],
                                            scalar1=column(3, g, h), scalar2=None, op0=ALU.mult)
                nc.sync.dma_start(out=out.rearrange("g (q h) n -> q g h n", h=2)[:, g, :, lo:hi],
                                  in_=res[k][:, g, :, :])

        for s in range(2):
            interleave("scalar", hh_bf[s], moved[s], HH_VECTOR_QUADS, NB // 4)
        quantize(woq[0], woq[1], wo_bf[:].rearrange("p b q j -> p (b q j)"), 0, O)
        for pair in ((0, 1), (2, 3)):
            for s in pair:
                interleave("vector", hh_bf[s], moved[s], 0, HH_VECTOR_QUADS if s < 2 else NB // 4)
            for s in pair:
                second_layer(s)
        for k in range(len(STORES)):
            store(k)
